import numpy as np
import ml_dtypes


def mxq(x, axis, fmt="e4m3"):
    dtype, down = {"e4m3": (ml_dtypes.float8_e4m3fn, 7), "e5m2": (ml_dtypes.float8_e5m2, 14)}[fmt]
    v = np.moveaxis(np.asarray(x, np.float32).astype(ml_dtypes.bfloat16).astype(np.float64), axis, -1)
    blocks = v.reshape(v.shape[:-1] + (-1, 32))
    amax = np.abs(blocks).max(-1, keepdims=True)
    byte = np.maximum(np.where(amax > 0, np.frexp(amax)[1] - 1 + 127, 0) - down, 1)
    scale = np.exp2(byte - 127.0)
    codes = (blocks / scale).astype(np.float32).astype(dtype).astype(np.float64)
    return np.moveaxis((codes * scale).reshape(v.shape), -1, axis)


WIDE = False


def mx_kscale(k):
    if not WIDE:
        return np.ones(k)
    levels = np.array([10, -10, 5, -5, 0])
    if k % 512:
        return np.exp2(np.random.permutation(np.resize(levels, k // 32))).repeat(32)
    a = np.empty((k // 512, 16))
    for p in range(k // 512):
        a[p, :8] = np.random.permutation(np.resize(levels, 8))
        for g in range(8):
            far = levels[np.abs(levels - a[p, g]) >= 10]
            a[p, g + 8] = far[np.random.randint(len(far))]
    return np.exp2(a.ravel()).repeat(32)


def f64(x):
    return np.asarray(x).astype(np.float64)


def striped(idx):
    return np.tile(idx.reshape(-1, 16).T, (8, 1)).astype(np.uint16)


def unstriped(offs):
    return offs[:16].T.reshape(-1).astype(np.int64)


def striped8(idx):
    return np.concatenate([x.reshape(-1, 16).T for x in idx]).astype(np.uint16)


def runs(offs, k):
    lists = np.stack([offs[16 * r : 16 * r + 16].T.reshape(-1) for r in range(8)]).astype(np.int64)
    return lists[np.arange(k) % 512 // 64]


def pack_weight(w):
    k, n = w.shape
    w = f64(np.asarray(w, np.float32).astype(ml_dtypes.bfloat16)).reshape(k // 32, 32, n)
    amax = np.abs(w).max(1)
    byte = np.clip(np.where(amax > 0, np.frexp(amax)[1] - 1 + 127 - 7, 1), 1, 254)
    scaled = (w * np.exp2(127.0 - byte)[:, None, :]).reshape(k, n).astype(np.float32)
    words = np.ascontiguousarray(scaled.reshape(k // 512, 128, 4, n).transpose(0, 1, 3, 2)).astype(ml_dtypes.float8_e4m3fn).view(np.uint8)
    return words, np.ascontiguousarray(byte.astype(np.uint8).reshape(k // 512, 16, n))


def unpack_weight(words, scales):
    g, p, n, _ = words.shape
    vals = np.ascontiguousarray(words).view(ml_dtypes.float8_e4m3fn).astype(np.float64) * np.repeat(np.exp2(scales.astype(np.float64) - 127.0), 8, axis=1)[..., None]
    return vals.transpose(0, 1, 3, 2).reshape(g * 512, n)


def sigmoid(v):
    return 1.0 / (1.0 + np.exp(-np.maximum(v, -700.0)))

def planes(y):
    n, m = y.shape
    v = y.astype(np.float32).astype(ml_dtypes.bfloat16).astype(np.float64).reshape(n // 32, 32, m)
    top = np.abs(v).max(1)
    byte = np.clip(np.where(top > 0, np.frexp(top)[1] - 1 + 127 - 7, 1), 1, 254)
    codes = (v * np.exp2(127.0 - byte)[:, None, :]).reshape(n, m).astype(np.float32).astype(ml_dtypes.float8_e4m3fn).view(np.uint8)
    words = codes.reshape(n // 512, 128, 4, m).transpose(0, 1, 3, 2)
    return np.ascontiguousarray(words), np.ascontiguousarray(byte.astype(np.uint8).reshape(n // 512, 16, m))


K, T, S, N, H = 512, 2048, 512, 512, 512


def setup_inputs():
    n = np.random.standard_normal
    s = mx_kscale(K)[:, None]
    u = mx_kscale(H)
    packed_xT = pack_weight(n((K, T)) * s)
    packed_w1 = pack_weight(n((K, H)) / np.sqrt(K) / s)
    packed_w2 = pack_weight(n((H, N)) / np.sqrt(H) / u[:, None])
    packed_w3 = pack_weight(n((K, N)) / np.sqrt(K) / s)
    return {
        "x_words": packed_xT[0],
        "x_scales": packed_xT[1],
        "w1_words": packed_w1[0],
        "w1_scales": packed_w1[1],
        "sl": np.random.uniform(1.5, 3.0, (H, 1)).astype(np.float32),
        "th": (0.5 * n((H, 1))).astype(np.float32),
        "gn": (np.random.uniform(0.5, 1.5, (H, 1)) * u[:, None]).astype(np.float32),
        "w2_words": packed_w2[0],
        "w2_scales": packed_w2[1],
        "w3_words": packed_w3[0],
        "w3_scales": packed_w3[1],
        "tau": np.random.uniform(0.3, 0.9, (N, 1)).astype(np.float32),
        "offs": striped(np.random.permutation(T)[:S]),
        "n1": striped8(np.stack([np.random.permutation(S) for _ in range(8)])),
        "n2": striped8(np.stack([np.random.permutation(S) for _ in range(8)])),
        "two": striped(np.random.permutation(T)[:S]),
        "n3": striped8(np.stack([np.random.permutation(S) for _ in range(8)])),
        "n4": striped8(np.stack([np.random.permutation(S) for _ in range(8)])),
    }


def reference(x_words, x_scales, w1_words, w1_scales, sl, th, gn, w2_words, w2_scales, w3_words, w3_scales, tau, offs, n1, n2, two, n3, n4):
    x_two = unpack_weight(x_words, x_scales)[:, unstriped(two)]
    d = unpack_weight(w3_words, w3_scales).T @ x_two
    top = d.max(axis=1, keepdims=True)
    ea = np.exp(f64(tau) * (d[np.arange(N)[:, None], runs(n3, N)] - top))
    xq = unpack_weight(x_words, x_scales)[:, unstriped(offs)]
    y = unpack_weight(w1_words, w1_scales).T @ xq
    sg = sigmoid(f64(sl) * (y[np.arange(H)[:, None], runs(n1, H)] - f64(th)))
    z = f64(gn) * (1.5 * (y * (sg - (sg[np.arange(H)[:, None], runs(n2, H)]))))
    h = unpack_weight(w2_words, w2_scales).T @ mxq(z, 0, "e4m3")
    out_0 = (2.0 * ea) * (h - (h[np.arange(N)[:, None], runs(n4, N)])) - (0.5 * d)
    return (out_0,) + planes(out_0)

@@ -1,0 +1,275 @@
+from contextlib import ExitStack
+
+import concourse.mybir as mybir
+
+F32 = mybir.dt.float32
+BF16 = mybir.dt.bfloat16
+U32 = mybir.dt.uint32
+I32 = mybir.dt.int32
+U16 = mybir.dt.uint16
+U8 = mybir.dt.uint8
+FP8X4 = mybir.dt.float8_e4m3fn_x4
+ALU = mybir.AluOpType
+ACT = mybir.ActivationFunctionType
+
+P = 128
+PACK = 4
+T = 2048
+S = 512
+HALF = S // 2
+LIST_COLS = S // 16
+FLOPS = 3 * 2 * 512 * 512 * 512
+
+
+def tile_picked_latepxbedb_none_po_kernel(
+    tc, x_words, x_scales, w1_words, w1_scales, sl, th, gn, w2_words, w2_scales, w3_words, w3_scales, tau,
+    offs, n1, n2, two, n3, n4, out_0, out_1, out_2,
+):
+    nc = tc.nc
+    tiles = range(PACK)
+    halves = range(2)
+
+    def cols(h):
+        return slice(h * HALF, (h + 1) * HALF)
+
+    def entries(lst, h):
+        return lst[:, h * LIST_COLS // 2 : (h + 1) * LIST_COLS // 2]
+
+    with ExitStack() as ctx:
+        keep = ctx.enter_context(tc.tile_pool(name="keep", bufs=1))
+        psum = ctx.enter_context(tc.psum_pool(name="psum", bufs=1))
+
+        def sb(name, shape, dtype):
+            return keep.tile(shape, dtype, name=name, align_bytes=64)
+
+        def load_list(name, src):
+            lst = sb(name, [P, LIST_COLS], U16)
+            nc.sync.dma_start(lst[:], src)
+            return lst
+
+        def load_words(name, src, width):
+            words = sb(name, [P, width], U32)
+            nc.sync.dma_start(words[:].bitcast(I32), src[0].rearrange("p n t -> p (n t)").bitcast(I32))
+            return words
+
+        def load_scale_rows(queue, plane, src, first):
+            for q in range(4):
+                queue.dma_start(
+                    plane[32 * q + first : 32 * q + first + 4, :].bitcast(I32),
+                    src[0, 4 * q : 4 * q + 4, :].bitcast(I32),
+                )
+
+        def load_scale_quadrants(plane, src):
+            width = src.shape[2] // 4
+            for q in range(4):
+                rows = src[0, 4 * q : 4 * q + 4, :].bitcast(I32)
+                nc.sync.dma_start(
+                    plane[32 * q : 32 * q + 32, :].bitcast(I32), rows.unsqueeze(0).to_broadcast([8, 4, width])
+                )
+
+        def load_rows(name, src):
+            vec = sb(name, [P, PACK], F32)
+            nc.gpsimd.dma_start(vec[:], src.rearrange("(p t) o -> p (t o)", t=PACK))
+            return vec
+
+        def deal(copy, dst, src):
+            copy(dst[:].rearrange("p (t m) -> p m t", t=PACK), src[:].rearrange("p (m t) -> p m t", t=PACK))
+
+        xs = sb("xs", [P, T], U8)
+        w1s_raw = sb("w1s_raw", [P, S], U8)
+        w3s_raw = sb("w3s_raw", [P, S], U8)
+        w2s_raw = sb("w2s_raw", [P, S], U8)
+        nc.vector.memset(w2s_raw[:].bitcast(I32), 0)
+        load_scale_quadrants(xs, x_scales)
+        offs_sb = load_list("offs_sb", offs)
+        xw = load_words("xw", x_words, T)
+        w1_raw = load_words("w1_raw", w1_words, S)
+        two_sb = load_list("two_sb", two)
+        sl_sb = load_rows("sl_sb", sl)
+        th_sb = load_rows("th_sb", th)
+        gn_sb = load_rows("gn_sb", gn)
+        tau_sb = load_rows("tau_sb", tau)
+        load_scale_quadrants(w1s_raw, w1_scales)
+        n1_sb = load_list("n1_sb", n1)
+        w3_raw = load_words("w3_raw", w3_words, S)
+        load_scale_quadrants(w3s_raw, w3_scales)
+        n2_sb = load_list("n2_sb", n2)
+        n3_sb = load_list("n3_sb", n3)
+        w2_raw = load_words("w2_raw", w2_words, S)
+        n4_sb = load_list("n4_sb", n4)
+        load_scale_rows(nc.sync, w2s_raw, w2_scales, 0)
+
+        xq_s = sb("xq_s", [P, S], U8)
+        xq_w = sb("xq_w", [P, S], U32)
+        x2_s = sb("x2_s", [P, S], U8)
+        x2_w = sb("x2_w", [P, S], U32)
+        w1 = sb("w1", [P, S], U32)
+        w2 = sb("w2", [P, S], U32)
+        w3 = sb("w3", [P, S], U32)
+        w1s = sb("w1s", [P, S], U8)
+        w3s = sb("w3s", [P, S], U8)
+        w2s = sb("w2s", [P, S], U8)
+        deal(nc.scalar.copy, w1, w1_raw)
+        nc.vector.tensor_copy(xq_s[:], xs[:].indirect(offs_sb[:]))
+        for h in halves:
+            nc.vector.tensor_copy(xq_w[:, cols(h)], xw[:].indirect(entries(offs_sb, h)))
+        deal(nc.vector.tensor_copy, w1s, w1s_raw)
+
+        sig_bias = sb("sig_bias", [P, PACK], F32)
+        gain = sb("gain", [P, PACK], F32)
+        ntau = sb("ntau", [P, PACK], F32)
+        nc.vector.scalar_tensor_tensor(sig_bias[:], sl_sb[:], -1.0, th_sb[:], ALU.mult, ALU.mult)
+        nc.vector.tensor_scalar(gain[:], gn_sb[:], -1.5, None, ALU.mult)
+        nc.vector.tensor_scalar(ntau[:], tau_sb[:], -1.0, None, ALU.mult)
+
+        def product(bank, w, ws, first, t, x, xsc, c):
+            m = slice(t * P, (t + 1) * P)
+            nc.tensor.matmul_mx(
+                out=bank[:, c], lhsT=w[:, m].bitcast(FP8X4), lhsT_scale=ws[first:P, m],
+                rhs=x[:, c].bitcast(FP8X4), rhs_scale=xsc[:, c], start=True, stop=True,
+            )
+
+        y_ps = [psum.tile([P, S], F32, name="yh_ps", tag=f"yh{t}") for t in tiles]
+        d_ps = [psum.tile([P, S], F32, name="d_ps", tag=f"d{t}") for t in tiles]
+        for h in halves:
+            product(y_ps[0], w1, w1s, 0, 0, xq_w, xq_s, cols(h))
+        for t in range(1, PACK):
+            product(y_ps[t], w1, w1s, 0, t, xq_w, xq_s, slice(0, S))
+
+        y = [sb(f"y{t}", [P, S], F32) for t in tiles]
+        sg = [sb(f"sg{t}", [P, S], F32) for t in tiles]
+        sg_again = [sb(f"sga{t}", [P, S], F32) for t in tiles]
+        u = [sb(f"u{t}", [P, S], F32) for t in tiles]
+        d = [sb(f"d{t}", [P, S], F32) for t in tiles]
+        z = sb("z", [P, PACK, S], BF16)
+        top = sb("top", [P, PACK], F32)
+        exp_bias = sb("exp_bias", [P, PACK], F32)
+
+        nc.vector.tensor_copy(y[0][:], y_ps[0][:])
+        for h in halves:
+            nc.vector.tensor_copy(x2_s[:, cols(h)], xs[:].indirect(entries(two_sb, h)))
+        for h in halves:
+            nc.vector.tensor_copy(x2_w[:, cols(h)], xw[:].indirect(entries(two_sb, h)))
+
+        def sigmoid_of(t):
+            for h in halves:
+                nc.scalar.activation(
+                    sg[t][:, cols(h)], y[t][:].indirect(entries(n1_sb, h)), ACT.Sigmoid,
+                    bias=sig_bias[:, t : t + 1], scale=sl_sb[:, t : t + 1],
+                )
+
+        sigmoid_of(0)
+        deal(nc.scalar.copy, w3, w3_raw)
+        deal(nc.vector.tensor_copy, w3s, w3s_raw)
+        for t in tiles:
+            product(d_ps[t], w3, w3s, 0, t, x2_w, x2_s, slice(0, S))
+
+        def d_out(t):
+            nc.vector.tensor_scalar(d[t][:], d_ps[t][:], 1.0, None, ALU.mult, ALU.max, accum_out=top[:, t : t + 1])
+
+        def diff_of(t):
+            nc.vector.tensor_copy(sg_again[t][:], sg[t][:])
+            for h in halves:
+                nc.vector.tensor_tensor(
+                    u[t][:, cols(h)], sg[t][:].indirect(entries(n2_sb, h)), sg_again[t][:, cols(h)], ALU.subtract
+                )
+
+        def z_of(t):
+            nc.vector.scalar_tensor_tensor(z[:, t, :], u[t][:], gain[:, t : t + 1], y[t][:], ALU.mult, ALU.mult)
+
+        for t in range(1, PACK):
+            nc.scalar.copy(y[t][:], y_ps[t][:])
+            sigmoid_of(t)
+        for t in tiles:
+            diff_of(t)
+            if t > 0:
+                z_of(t - 1)
+            if t < 2:
+                d_out(t)
+        nc.vector.tensor_tensor(exp_bias[:, 0:2], top[:, 0:2], ntau[:, 0:2], ALU.mult)
+        z_of(PACK - 1)
+
+        z4 = sb("z4", [P, S * PACK], BF16)
+        zw = sb("zw", [P, S], U32)
+        zs = sb("zs", [P, S], U8)
+
+        def weave(copy, dst, src, c0, c1):
+            copy(
+                dst[:, PACK * c0 : PACK * c1].rearrange("p (c i t) -> p c t i", i=4, t=PACK),
+                src[:, :, c0:c1].rearrange("p t (c i) -> p c t i", i=4),
+            )
+
+        def quantise(words, plane, src, h):
+            nc.vector.quantize_mx(
+                out=words[:, cols(h)].bitcast(FP8X4), scales=plane[:, cols(h)],
+                in_=src[:, PACK * h * HALF : PACK * (h + 1) * HALF],
+            )
+
+        deal(nc.scalar.copy, w2, w2_raw)
+        deal(nc.vector.tensor_copy, w2s, w2s_raw)
+        for h in halves:
+            weave(nc.vector.tensor_copy, z4, z, h * HALF, (h + 1) * HALF)
+        for h in halves:
+            quantise(zw, zs, z4, h)
+        d_out(2)
+        d_out(3)
+        nc.vector.tensor_tensor(exp_bias[:, 2:4], top[:, 2:4], ntau[:, 2:4], ALU.mult)
+
+        h_ps = [psum.tile([P, S], F32, name="yh_ps", tag=f"yh{t}") for t in tiles]
+        for h in halves:
+            product(h_ps[0], w2, w2s, 0, 0, zw, zs, cols(h))
+        for t in range(1, PACK):
+            product(h_ps[t], w2, w2s, 0, t, zw, zs, slice(0, S))
+
+        ea = [sb(f"ea{t}", [P, S], F32) for t in tiles]
+        hh = [sb(f"h{t}", [P, S], F32) for t in tiles]
+        hg = [sb(f"hg{t}", [P, S], F32) for t in tiles]
+        v = [sb(f"v{t}", [P, S], F32) for t in tiles]
+        m = [sb(f"m{t}", [P, S], F32) for t in tiles]
+        res = sb("res", [P, PACK, S], F32)
+        res4 = sb("res4", [P, S * PACK], BF16)
+        ow = sb("ow", [P, S], U32)
+        osc = sb("osc", [P, S], U8)
+        out_rows = out_0.rearrange("(p t) j -> p t j", t=PACK)
+
+        def exp_of(t, h):
+            nc.scalar.activation(
+                ea[t][:, cols(h)], d[t][:].indirect(entries(n3_sb, h)), ACT.Exp,
+                bias=exp_bias[:, t : t + 1], scale=tau_sb[:, t : t + 1],
+            )
+
+        def fetch_h(t, h):
+            nc.scalar.activation(hg[t][:, cols(h)], hh[t][:].indirect(entries(n4_sb, h)), ACT.Copy)
+
+        for t in range(2):
+            for h in halves:
+                exp_of(t, h)
+        for t in tiles:
+            nc.scalar.copy(hh[t][:], h_ps[t][:])
+            fetch_h(t, 0)
+            if t >= 2:
+                exp_of(t, 0)
+        for t in tiles:
+            fetch_h(t, 1)
+            if t >= 2:
+                exp_of(t, 1)
+
+        for h in halves:
+            c = cols(h)
+            for pair in range(2):
+                ts = (2 * pair, 2 * pair + 1)
+                for t in ts:
+                    nc.vector.tensor_tensor(v[t][:, c], hh[t][:, c], hg[t][:, c], ALU.subtract)
+                for t in ts:
+                    nc.vector.scalar_tensor_tensor(m[t][:, c], v[t][:, c], 2.0, ea[t][:, c], ALU.mult, ALU.mult)
+                for t in ts:
+                    nc.vector.scalar_tensor_tensor(res[:, t, c], d[t][:, c], -0.5, m[t][:, c], ALU.mult, ALU.add)
+                nc.sync.dma_start(out_rows[:, ts[0] : ts[1] + 1, c], res[:, ts[0] : ts[1] + 1, c])
+            weave(nc.vector.tensor_copy, res4, res, h * HALF, (h + 1) * HALF)
+            quantise(ow, osc, res4, h)
+            nc.sync.dma_start(
+                out_1[0].rearrange("p n t -> p (n t)").bitcast(I32)[:, c], ow[:, c].bitcast(I32)
+            )
+        for q in range(4):
+            queue = nc.sync if q % 2 else nc.scalar
+            queue.dma_start(out_2[0, 4 * q : 4 * q + 4, :].bitcast(I32), osc[32 * q : 32 * q + 4, :].bitcast(I32))

@@ -18,6 +18,7 @@ T = 2048
 S = 512
 HALF = S // 2
 LIST_COLS = S // 16
+SPLIT = 416
 FLOPS = 3 * 2 * 512 * 512 * 512
 
 
@@ -32,8 +33,13 @@ def tile_picked_latepxbedb_none_po_kernel(
     def cols(h):
         return slice(h * HALF, (h + 1) * HALF)
 
-    def entries(lst, h):
-        return lst[:, h * LIST_COLS // 2 : (h + 1) * LIST_COLS // 2]
+    def entries(lst, c):
+        return lst[:, c.start // 16 : c.stop // 16]
+
+    def spare(c):
+        return slice(S + c.start, S + c.stop)
+
+    whole = slice(0, S)
 
     with ExitStack() as ctx:
         keep = ctx.enter_context(tc.tile_pool(name="keep", bufs=1))
@@ -52,177 +58,172 @@ def tile_picked_latepxbedb_none_po_kernel(
             nc.sync.dma_start(words[:].bitcast(I32), src[0].rearrange("p n t -> p (n t)").bitcast(I32))
             return words
 
-        def load_scale_rows(queue, plane, src, first):
-            for q in range(4):
-                queue.dma_start(
-                    plane[32 * q + first : 32 * q + first + 4, :].bitcast(I32),
-                    src[0, 4 * q : 4 * q + 4, :].bitcast(I32),
-                )
-
-        def load_scale_quadrants(plane, src):
-            width = src.shape[2] // 4
+        def load_scale_quadrants(name, src, width):
+            plane = sb(name, [P, width], U8)
             for q in range(4):
                 rows = src[0, 4 * q : 4 * q + 4, :].bitcast(I32)
                 nc.sync.dma_start(
-                    plane[32 * q : 32 * q + 32, :].bitcast(I32), rows.unsqueeze(0).to_broadcast([8, 4, width])
+                    plane[32 * q : 32 * q + 32, :].bitcast(I32), rows.unsqueeze(0).to_broadcast([8, 4, width // 4])
                 )
+            return plane
 
         def load_rows(name, src):
             vec = sb(name, [P, PACK], F32)
-            nc.gpsimd.dma_start(vec[:], src.rearrange("(p t) o -> p (t o)", t=PACK))
+            nc.sync.dma_start(vec[:], src.rearrange("(p t) o -> p (t o)", t=PACK))
             return vec
 
-        def deal(copy, dst, src):
-            copy(dst[:].rearrange("p (t m) -> p m t", t=PACK), src[:].rearrange("p (m t) -> p m t", t=PACK))
+        def deal(copy, name, src, dtype):
+            dst = sb(name, [P, S], dtype)
+            copy(dst[:].rearrange("p (t m) -> p t m", t=PACK), src[:].rearrange("p (m t) -> p t m", t=PACK))
+            return dst
 
-        xs = sb("xs", [P, T], U8)
-        w1s_raw = sb("w1s_raw", [P, S], U8)
-        w3s_raw = sb("w3s_raw", [P, S], U8)
-        w2s_raw = sb("w2s_raw", [P, S], U8)
-        nc.vector.memset(w2s_raw[:].bitcast(I32), 0)
-        load_scale_quadrants(xs, x_scales)
+        def window(name):
+            return sb(name, [P, 2 * S], F32)
+
+        y = [window(f"y{t}") for t in tiles]
+        sg = [window(f"sg{t}") for t in tiles]
+        for t in tiles:
+            nc.vector.memset(y[t][:, S:], 0.0)
+            nc.gpsimd.memset(sg[t][:, S:], 0.0)
+        xs = load_scale_quadrants("xs", x_scales, T)
         offs_sb = load_list("offs_sb", offs)
-        xw = load_words("xw", x_words, T)
-        w1_raw = load_words("w1_raw", w1_words, S)
         two_sb = load_list("two_sb", two)
+        w1_raw = load_words("w1_raw", w1_words, S)
+        xw = load_words("xw", x_words, T)
+        w1s_raw = load_scale_quadrants("w1s_raw", w1_scales, S)
         sl_sb = load_rows("sl_sb", sl)
         th_sb = load_rows("th_sb", th)
-        gn_sb = load_rows("gn_sb", gn)
-        tau_sb = load_rows("tau_sb", tau)
-        load_scale_quadrants(w1s_raw, w1_scales)
         n1_sb = load_list("n1_sb", n1)
         w3_raw = load_words("w3_raw", w3_words, S)
-        load_scale_quadrants(w3s_raw, w3_scales)
+        w3s_raw = load_scale_quadrants("w3s_raw", w3_scales, S)
+        gn_sb = load_rows("gn_sb", gn)
         n2_sb = load_list("n2_sb", n2)
-        n3_sb = load_list("n3_sb", n3)
+        tau_sb = load_rows("tau_sb", tau)
         w2_raw = load_words("w2_raw", w2_words, S)
+        w2s_raw = load_scale_quadrants("w2s_raw", w2_scales, S)
+        n3_sb = load_list("n3_sb", n3)
         n4_sb = load_list("n4_sb", n4)
-        load_scale_rows(nc.sync, w2s_raw, w2_scales, 0)
 
+        last = PACK - 1
         xq_s = sb("xq_s", [P, S], U8)
         xq_w = sb("xq_w", [P, S], U32)
         x2_s = sb("x2_s", [P, S], U8)
         x2_w = sb("x2_w", [P, S], U32)
-        w1 = sb("w1", [P, S], U32)
-        w2 = sb("w2", [P, S], U32)
-        w3 = sb("w3", [P, S], U32)
-        w1s = sb("w1s", [P, S], U8)
-        w3s = sb("w3s", [P, S], U8)
-        w2s = sb("w2s", [P, S], U8)
-        deal(nc.scalar.copy, w1, w1_raw)
+        w1 = deal(nc.scalar.copy, "w1", w1_raw, U32)
         nc.vector.tensor_copy(xq_s[:], xs[:].indirect(offs_sb[:]))
+        nc.vector.tensor_copy(x2_s[:], xs[:].indirect(two_sb[:]))
         for h in halves:
-            nc.vector.tensor_copy(xq_w[:, cols(h)], xw[:].indirect(entries(offs_sb, h)))
-        deal(nc.vector.tensor_copy, w1s, w1s_raw)
+            nc.vector.tensor_copy(xq_w[:, cols(h)], xw[:].indirect(entries(offs_sb, cols(h))))
+        nc.vector.tensor_copy(x2_w[:], xw[:].indirect(two_sb[:]))
 
+        neg_th = sb("neg_th", [P, PACK], F32)
         sig_bias = sb("sig_bias", [P, PACK], F32)
         gain = sb("gain", [P, PACK], F32)
-        ntau = sb("ntau", [P, PACK], F32)
-        nc.vector.scalar_tensor_tensor(sig_bias[:], sl_sb[:], -1.0, th_sb[:], ALU.mult, ALU.mult)
-        nc.vector.tensor_scalar(gain[:], gn_sb[:], -1.5, None, ALU.mult)
-        nc.vector.tensor_scalar(ntau[:], tau_sb[:], -1.0, None, ALU.mult)
+        neg_tau = sb("neg_tau", [P, PACK], F32)
+        w1s = []
+        for t in tiles:
+            w1s.append(sb(f"w1s_{t}", [P, P], U8))
+            nc.gpsimd.tensor_copy(w1s[t][:], w1s_raw[:, t : S : PACK])
+            if t == 0:
+                nc.gpsimd.tensor_scalar(neg_th[:], th_sb[:], -1.0, 0.0, ALU.mult, ALU.add)
+                nc.gpsimd.tensor_tensor(sig_bias[:], neg_th[:], sl_sb[:], ALU.mult)
+        w3 = deal(nc.gpsimd.tensor_copy, "w3", w3_raw, U32)
+        nc.gpsimd.tensor_scalar(gain[:], gn_sb[:], -1.5, 0.0, ALU.mult, ALU.add)
+        nc.gpsimd.tensor_scalar(neg_tau[:], tau_sb[:], -1.0, 0.0, ALU.mult, ALU.add)
 
-        def product(bank, w, ws, first, t, x, xsc, c):
-            m = slice(t * P, (t + 1) * P)
+        def rows_of(t):
+            return slice(t * P, (t + 1) * P)
+
+        def product(out, w, ws, x, xsc):
             nc.tensor.matmul_mx(
-                out=bank[:, c], lhsT=w[:, m].bitcast(FP8X4), lhsT_scale=ws[first:P, m],
-                rhs=x[:, c].bitcast(FP8X4), rhs_scale=xsc[:, c], start=True, stop=True,
+                out=out, lhsT=w.bitcast(FP8X4), lhsT_scale=ws,
+                rhs=x.bitcast(FP8X4), rhs_scale=xsc, start=True, stop=True,
             )
 
-        y_ps = [psum.tile([P, S], F32, name="yh_ps", tag=f"yh{t}") for t in tiles]
-        d_ps = [psum.tile([P, S], F32, name="d_ps", tag=f"d{t}") for t in tiles]
-        for h in halves:
-            product(y_ps[0], w1, w1s, 0, 0, xq_w, xq_s, cols(h))
-        for t in range(1, PACK):
-            product(y_ps[t], w1, w1s, 0, t, xq_w, xq_s, slice(0, S))
-
-        y = [sb(f"y{t}", [P, S], F32) for t in tiles]
-        sg = [sb(f"sg{t}", [P, S], F32) for t in tiles]
-        sg_again = [sb(f"sga{t}", [P, S], F32) for t in tiles]
-        u = [sb(f"u{t}", [P, S], F32) for t in tiles]
-        d = [sb(f"d{t}", [P, S], F32) for t in tiles]
         z = sb("z", [P, PACK, S], BF16)
-        top = sb("top", [P, PACK], F32)
-        exp_bias = sb("exp_bias", [P, PACK], F32)
+        d = [window(f"d{t}") for t in tiles]
+        hh = {t: window(f"h{t}") for t in (0, 1, last)}
 
-        nc.vector.tensor_copy(y[0][:], y_ps[0][:])
+        y_ps = [psum.tile([P, S], F32, name="y_ps", tag=f"yh{t}") for t in range(2)]
         for h in halves:
-            nc.vector.tensor_copy(x2_s[:, cols(h)], xs[:].indirect(entries(two_sb, h)))
-        for h in halves:
-            nc.vector.tensor_copy(x2_w[:, cols(h)], xw[:].indirect(entries(two_sb, h)))
-
-        def sigmoid_of(t):
-            for h in halves:
-                nc.scalar.activation(
-                    sg[t][:, cols(h)], y[t][:].indirect(entries(n1_sb, h)), ACT.Sigmoid,
-                    bias=sig_bias[:, t : t + 1], scale=sl_sb[:, t : t + 1],
-                )
-
-        sigmoid_of(0)
-        deal(nc.scalar.copy, w3, w3_raw)
-        deal(nc.vector.tensor_copy, w3s, w3s_raw)
+            product(y_ps[0][:, cols(h)], w1[:, rows_of(0)], w1s[0][:], xq_w[:, cols(h)], xq_s[:, cols(h)])
+        product(y_ps[1][:], w1[:, rows_of(1)], w1s[1][:], xq_w[:], xq_s[:])
+        nc.scalar.copy(y[0][:, whole], y_ps[0][:])
+        nc.vector.tensor_copy(y[1][:, whole], y_ps[1][:])
         for t in tiles:
-            product(d_ps[t], w3, w3s, 0, t, x2_w, x2_s, slice(0, S))
-
-        def d_out(t):
-            nc.vector.tensor_scalar(d[t][:], d_ps[t][:], 1.0, None, ALU.mult, ALU.max, accum_out=top[:, t : t + 1])
-
-        def diff_of(t):
-            nc.vector.tensor_copy(sg_again[t][:], sg[t][:])
-            for h in halves:
-                nc.vector.tensor_tensor(
-                    u[t][:, cols(h)], sg[t][:].indirect(entries(n2_sb, h)), sg_again[t][:, cols(h)], ALU.subtract
-                )
-
-        def z_of(t):
-            nc.vector.scalar_tensor_tensor(z[:, t, :], u[t][:], gain[:, t : t + 1], y[t][:], ALU.mult, ALU.mult)
-
-        for t in range(1, PACK):
-            nc.scalar.copy(y[t][:], y_ps[t][:])
-            sigmoid_of(t)
-        for t in tiles:
-            diff_of(t)
-            if t > 0:
-                z_of(t - 1)
+            nc.scalar.activation(
+                sg[t][:, whole], y[t][:].indirect(n1_sb[:]), ACT.Sigmoid,
+                bias=sig_bias[:, t : t + 1], scale=sl_sb[:, t : t + 1],
+            )
             if t < 2:
-                d_out(t)
-        nc.vector.tensor_tensor(exp_bias[:, 0:2], top[:, 0:2], ntau[:, 0:2], ALU.mult)
-        z_of(PACK - 1)
+                bank = psum.tile([P, S], F32, name="y_ps", tag=f"yh{t}")
+                product(bank[:], w1[:, rows_of(t + 2)], w1s[t + 2][:], xq_w[:], xq_s[:])
+                nc.scalar.copy(y[t + 2][:, whole], bank[:])
+        hh[2] = window("sig_bias")
+        for t, c in ((2, whole), (last, cols(0)), (last, cols(1))):
+            nc.scalar.activation(hh[t][:, spare(c)], sg[t][:].indirect(entries(n2_sb, c)), ACT.Copy)
+
+        w3s = deal(nc.gpsimd.tensor_copy, "w1", w3s_raw, U8)
+        w2 = deal(nc.gpsimd.tensor_copy, "w3s_raw", w2_raw, U32)
+        w2s = deal(nc.gpsimd.tensor_copy, "w2_raw", w2s_raw, U8)
+        d_ps = [psum.tile([P, S], F32, name="d_ps", tag=f"d{t}") for t in tiles]
+        for t in tiles:
+            product(d_ps[t][:], w3[:, rows_of(t)], w3s[:, rows_of(t)], x2_w[:], x2_s[:])
 
         z4 = sb("z4", [P, S * PACK], BF16)
         zw = sb("zw", [P, S], U32)
         zs = sb("zs", [P, S], U8)
 
-        def weave(copy, dst, src, c0, c1):
+        def weave(copy, dst, c, src):
             copy(
-                dst[:, PACK * c0 : PACK * c1].rearrange("p (c i t) -> p c t i", i=4, t=PACK),
-                src[:, :, c0:c1].rearrange("p t (c i) -> p c t i", i=4),
+                dst[:, PACK * c.start : PACK * c.stop].rearrange("p (c i t) -> p c t i", i=4, t=PACK),
+                src[:, :, c].rearrange("p t (c i) -> p c t i", i=4),
             )
 
-        def quantise(words, plane, src, h):
+        def quantise(words, plane, src, c):
             nc.vector.quantize_mx(
-                out=words[:, cols(h)].bitcast(FP8X4), scales=plane[:, cols(h)],
-                in_=src[:, PACK * h * HALF : PACK * (h + 1) * HALF],
+                out=words[:, c].bitcast(FP8X4), scales=plane[:, c], in_=src[:, PACK * c.start : PACK * c.stop]
             )
 
-        deal(nc.scalar.copy, w2, w2_raw)
-        deal(nc.vector.tensor_copy, w2s, w2s_raw)
-        for h in halves:
-            weave(nc.vector.tensor_copy, z4, z, h * HALF, (h + 1) * HALF)
-        for h in halves:
-            quantise(zw, zs, z4, h)
-        d_out(2)
-        d_out(3)
-        nc.vector.tensor_tensor(exp_bias[:, 2:4], top[:, 2:4], ntau[:, 2:4], ALU.mult)
+        def gate_difference(t, c):
+            nc.vector.tensor_tensor(d[t][:, spare(c)], hh[t][:, spare(c)], sg[t][:, c], ALU.subtract)
 
-        h_ps = [psum.tile([P, S], F32, name="yh_ps", tag=f"yh{t}") for t in tiles]
-        for h in halves:
-            product(h_ps[0], w2, w2s, 0, 0, zw, zs, cols(h))
-        for t in range(1, PACK):
-            product(h_ps[t], w2, w2s, 0, t, zw, zs, slice(0, S))
+        def z_of(t, c):
+            nc.vector.scalar_tensor_tensor(
+                z[:, t, c], d[t][:, spare(c)], gain[:, t : t + 1], y[t][:, c], ALU.mult, ALU.mult
+            )
 
-        ea = [sb(f"ea{t}", [P, S], F32) for t in tiles]
-        hh = [sb(f"h{t}", [P, S], F32) for t in tiles]
+        for t in range(2):
+            nc.vector.tensor_copy(hh[t][:, S:], sg[t][:, whole])
+            nc.vector.tensor_tensor(d[t][:, S:], sg[t][:].indirect(n2_sb[:]), hh[t][:, S:], ALU.subtract)
+            z_of(t, whole)
+        gate_difference(2, whole)
+        gate_difference(last, cols(0))
+        z_of(2, whole)
+        z_of(last, cols(0))
+        gate_difference(last, cols(1))
+        weave(nc.vector.tensor_copy, z4, cols(0), z)
+        z_of(last, cols(1))
+        quantise(zw, zs, z4, cols(0))
+        weave(nc.vector.tensor_copy, z4, cols(1), z)
+        quantise(zw, zs, z4, cols(1))
+
+        top = sb("top", [P, last], F32)
+        last_top = sb("z", [P, 1], F32)
+        exp_bias = sb("exp_bias", [P, PACK], F32)
+        for t in tiles:
+            largest = top[:, t : t + 1] if t < last else last_top[:]
+            nc.vector.tensor_scalar(d[t][:, whole], d_ps[t][:], 1.0, None, ALU.mult, ALU.max, accum_out=largest)
+            if t == last - 1:
+                nc.vector.tensor_tensor(exp_bias[:, :last], top[:], neg_tau[:, :last], ALU.mult)
+        nc.vector.tensor_tensor(exp_bias[:, last:], last_top[:], neg_tau[:, last:], ALU.mult)
+
+        h_ps = [psum.tile([P, S], F32, name="h_ps", tag=f"yh{t}") for t in tiles]
+        for t in tiles:
+            for h in halves:
+                product(h_ps[t][:, cols(h)], w2[:, rows_of(t)], w2s[:, rows_of(t)], zw[:, cols(h)], zs[:, cols(h)])
+
+        ea = [sb(tag, [P, S], F32) for tag in ("sl_sb", "sg2", "ea2", "ea3")]
         hg = [sb(f"hg{t}", [P, S], F32) for t in tiles]
         v = [sb(f"v{t}", [P, S], F32) for t in tiles]
         m = [sb(f"m{t}", [P, S], F32) for t in tiles]
@@ -232,44 +233,57 @@ def tile_picked_latepxbedb_none_po_kernel(
         osc = sb("osc", [P, S], U8)
         out_rows = out_0.rearrange("(p t) j -> p t j", t=PACK)
 
-        def exp_of(t, h):
+        def exp_of(t, c):
             nc.scalar.activation(
-                ea[t][:, cols(h)], d[t][:].indirect(entries(n3_sb, h)), ACT.Exp,
+                ea[t][:, c], d[t][:].indirect(entries(n3_sb, c)), ACT.Exp,
                 bias=exp_bias[:, t : t + 1], scale=tau_sb[:, t : t + 1],
             )
 
-        def fetch_h(t, h):
-            nc.scalar.activation(hg[t][:, cols(h)], hh[t][:].indirect(entries(n4_sb, h)), ACT.Copy)
+        def fetch(t, c):
+            nc.scalar.activation(hg[t][:, c], hh[t][:].indirect(entries(n4_sb, c)), ACT.Copy)
+
+        def difference(t, c):
+            nc.vector.scalar_tensor_tensor(v[t][:, c], h_ps[t][:, c], 2.0, hg[t][:, c], ALU.mult, ALU.add)
+
+        def weigh(t, c):
+            nc.gpsimd.tensor_tensor(m[t][:, c], v[t][:, c], ea[t][:, c], ALU.mult)
+
+        def finish(t, c):
+            nc.vector.scalar_tensor_tensor(res[:, t, c], d_ps[t][:, c], -0.5, m[t][:, c], ALU.mult, ALU.add)
+
+        def hand_on(c):
+            quantise(ow, osc, res4, c)
+            nc.sync.dma_start(out_1[0].rearrange("p n t -> p (n t)").bitcast(I32)[:, c], ow[:, c].bitcast(I32))
 
         for t in range(2):
-            for h in halves:
-                exp_of(t, h)
-        for t in tiles:
-            nc.scalar.copy(hh[t][:], h_ps[t][:])
-            fetch_h(t, 0)
-            if t >= 2:
-                exp_of(t, 0)
-        for t in tiles:
-            fetch_h(t, 1)
-            if t >= 2:
-                exp_of(t, 1)
-
+            exp_of(t, whole)
+        nc.vector.tensor_scalar(hh[0][:, whole], h_ps[0][:], -2.0, None, ALU.mult)
+        nc.scalar.activation(hh[1][:, whole], h_ps[1][:], ACT.Copy, scale=-2.0)
+        fetch(1, whole)
+        nc.vector.tensor_scalar(hh[2][:, whole], h_ps[2][:], -2.0, None, ALU.mult)
+        nc.vector.tensor_copy(hg[0][:], hh[0][:, whole])
+        nc.vector.tensor_scalar(hh[3][:, whole], h_ps[3][:], -2.0, None, ALU.mult)
+        nc.vector.tensor_tensor(v[0][:], hh[0][:].indirect(n4_sb[:]), hg[0][:], ALU.subtract)
         for h in halves:
-            c = cols(h)
-            for pair in range(2):
-                ts = (2 * pair, 2 * pair + 1)
-                for t in ts:
-                    nc.vector.tensor_tensor(v[t][:, c], hh[t][:, c], hg[t][:, c], ALU.subtract)
-                for t in ts:
-                    nc.vector.scalar_tensor_tensor(m[t][:, c], v[t][:, c], 2.0, ea[t][:, c], ALU.mult, ALU.mult)
-                for t in ts:
-                    nc.vector.scalar_tensor_tensor(res[:, t, c], d[t][:, c], -0.5, m[t][:, c], ALU.mult, ALU.add)
-                nc.sync.dma_start(out_rows[:, ts[0] : ts[1] + 1, c], res[:, ts[0] : ts[1] + 1, c])
-            weave(nc.vector.tensor_copy, res4, res, h * HALF, (h + 1) * HALF)
-            quantise(ow, osc, res4, h)
-            nc.sync.dma_start(
-                out_1[0].rearrange("p n t -> p (n t)").bitcast(I32)[:, c], ow[:, c].bitcast(I32)
-            )
+            for step in (fetch, exp_of):
+                for t in (2, 3):
+                    step(t, cols(h))
+        weigh(0, whole)
+        difference(1, whole)
+        weigh(1, whole)
+        for t in range(2):
+            finish(t, whole)
+        nc.sync.dma_start(out_rows[:, 0:2, :], res[:, 0:2, :])
+        for h in halves:
+            for step in (difference, weigh, finish):
+                for t in (2, 3):
+                    step(t, cols(h))
+            nc.sync.dma_start(out_rows[:, 2:4, cols(h)], res[:, 2:4, cols(h)])
+        weave(nc.scalar.copy, res4, cols(0), res)
+        hand_on(cols(0))
+        weave(nc.vector.tensor_copy, res4, slice(HALF, SPLIT), res)
+        weave(nc.scalar.copy, res4, slice(SPLIT, S), res)
+        hand_on(cols(1))
         for q in range(4):
             queue = nc.sync if q % 2 else nc.scalar
             queue.dma_start(out_2[0, 4 * q : 4 * q + 4, :].bitcast(I32), osc[32 * q : 32 * q + 4, :].bitcast(I32))

@@ -14,10 +14,12 @@ ACT = mybir.ActivationFunctionType
 
 P = 128
 PACK = 4
+LAST = PACK - 1
 T = 2048
 S = 512
 HALF = S // 2
-LIST_COLS = S // 16
+QUADRANT = 32
+PER_COLUMN = 16
 SPLIT = 416
 FLOPS = 3 * 2 * 512 * 512 * 512
 
@@ -27,19 +29,18 @@ def tile_picked_latepxbedb_none_po_kernel(
     offs, n1, n2, two, n3, n4, out_0, out_1, out_2,
 ):
     nc = tc.nc
-    tiles = range(PACK)
-    halves = range(2)
-
-    def cols(h):
-        return slice(h * HALF, (h + 1) * HALF)
+    row_tiles = range(PACK)
+    whole = slice(0, S)
+    halves = (slice(0, HALF), slice(HALF, S))
 
     def entries(lst, c):
-        return lst[:, c.start // 16 : c.stop // 16]
+        return lst[:, c.start // PER_COLUMN : c.stop // PER_COLUMN]
 
     def spare(c):
         return slice(S + c.start, S + c.stop)
 
-    whole = slice(0, S)
+    def rows_of(t):
+        return slice(t * P, (t + 1) * P)
 
     with ExitStack() as ctx:
         keep = ctx.enter_context(tc.tile_pool(name="keep", bufs=1))
@@ -48,8 +49,14 @@ def tile_picked_latepxbedb_none_po_kernel(
         def sb(name, shape, dtype):
             return keep.tile(shape, dtype, name=name, align_bytes=64)
 
+        def bank(name, width=S):
+            return psum.tile([P, width], F32, name=name)
+
+        def window(name):
+            return sb(name, [P, 2 * S], F32)
+
         def load_list(name, src):
-            lst = sb(name, [P, LIST_COLS], U16)
+            lst = sb(name, [P, S // PER_COLUMN], U16)
             nc.sync.dma_start(lst[:], src)
             return lst
 
@@ -58,12 +65,13 @@ def tile_picked_latepxbedb_none_po_kernel(
             nc.sync.dma_start(words[:].bitcast(I32), src[0].rearrange("p n t -> p (n t)").bitcast(I32))
             return words
 
-        def load_scale_quadrants(name, src, width):
+        def load_scales(name, src, width):
             plane = sb(name, [P, width], U8)
-            for q in range(4):
+            for q in range(P // QUADRANT):
                 rows = src[0, 4 * q : 4 * q + 4, :].bitcast(I32)
                 nc.sync.dma_start(
-                    plane[32 * q : 32 * q + 32, :].bitcast(I32), rows.unsqueeze(0).to_broadcast([8, 4, width // 4])
+                    plane[QUADRANT * q : QUADRANT * (q + 1), :].bitcast(I32),
+                    rows.unsqueeze(0).to_broadcast([QUADRANT // 4, 4, width // 4]),
                 )
             return plane
 
@@ -74,37 +82,51 @@ def tile_picked_latepxbedb_none_po_kernel(
 
         def deal(copy, name, src, dtype):
             dst = sb(name, [P, S], dtype)
-            copy(dst[:].rearrange("p (t m) -> p t m", t=PACK), src[:].rearrange("p (m t) -> p t m", t=PACK))
+            walk = "p m t" if dtype == U32 else "p t m"
+            copy(dst[:].rearrange(f"p (t m) -> {walk}", t=PACK), src[:].rearrange(f"p (m t) -> {walk}", t=PACK))
             return dst
 
-        def window(name):
-            return sb(name, [P, 2 * S], F32)
+        def product(out, w, w_scale, x, x_scale):
+            nc.tensor.matmul_mx(
+                out=out, lhsT=w.bitcast(FP8X4), lhsT_scale=w_scale,
+                rhs=x.bitcast(FP8X4), rhs_scale=x_scale, start=True, stop=True,
+            )
 
-        y = [window(f"y{t}") for t in tiles]
-        sg = [window(f"sg{t}") for t in tiles]
-        for t in tiles:
-            nc.vector.memset(y[t][:, S:], 0.0)
-            nc.gpsimd.memset(sg[t][:, S:], 0.0)
-        xs = load_scale_quadrants("xs", x_scales, T)
+        def weave(copy, dst, src, c):
+            copy(
+                dst[:, PACK * c.start : PACK * c.stop].rearrange("p (c i t) -> p c t i", i=4, t=PACK),
+                src[:, :, c].rearrange("p t (c i) -> p c t i", i=4),
+            )
+
+        def quantise(words, plane, woven, c):
+            nc.vector.quantize_mx(
+                out=words[:, c].bitcast(FP8X4), scales=plane[:, c], in_=woven[:, PACK * c.start : PACK * c.stop]
+            )
+
+        y = [window(f"y{t}") for t in row_tiles]
+        sg = [window(f"sg{t}") for t in range(LAST)] + [sb("sg3", [P, S], F32)]
+        for tile in y + sg[:LAST]:
+            nc.vector.memset(tile[:, S:], 0.0)
+
+        xs = load_scales("xs", x_scales, T)
         offs_sb = load_list("offs_sb", offs)
         two_sb = load_list("two_sb", two)
         w1_raw = load_words("w1_raw", w1_words, S)
         xw = load_words("xw", x_words, T)
-        w1s_raw = load_scale_quadrants("w1s_raw", w1_scales, S)
+        w1s_raw = load_scales("w1s_raw", w1_scales, S)
         sl_sb = load_rows("sl_sb", sl)
         th_sb = load_rows("th_sb", th)
-        n1_sb = load_list("n1_sb", n1)
         w3_raw = load_words("w3_raw", w3_words, S)
-        w3s_raw = load_scale_quadrants("w3s_raw", w3_scales, S)
+        n1_sb = load_list("n1_sb", n1)
+        w3s_raw = load_scales("w3s_raw", w3_scales, S)
         gn_sb = load_rows("gn_sb", gn)
         n2_sb = load_list("n2_sb", n2)
         tau_sb = load_rows("tau_sb", tau)
         w2_raw = load_words("w2_raw", w2_words, S)
-        w2s_raw = load_scale_quadrants("w2s_raw", w2_scales, S)
+        w2s_raw = load_scales("w2s_raw", w2_scales, S)
         n3_sb = load_list("n3_sb", n3)
         n4_sb = load_list("n4_sb", n4)
 
-        last = PACK - 1
         xq_s = sb("xq_s", [P, S], U8)
         xq_w = sb("xq_w", [P, S], U32)
         x2_s = sb("x2_s", [P, S], U8)
@@ -112,125 +134,104 @@ def tile_picked_latepxbedb_none_po_kernel(
         w1 = deal(nc.scalar.copy, "w1", w1_raw, U32)
         nc.vector.tensor_copy(xq_s[:], xs[:].indirect(offs_sb[:]))
         nc.vector.tensor_copy(x2_s[:], xs[:].indirect(two_sb[:]))
-        for h in halves:
-            nc.vector.tensor_copy(xq_w[:, cols(h)], xw[:].indirect(entries(offs_sb, cols(h))))
-        nc.vector.tensor_copy(x2_w[:], xw[:].indirect(two_sb[:]))
-
-        neg_th = sb("neg_th", [P, PACK], F32)
+        nc.vector.tensor_copy(xq_w[:, halves[0]], xw[:].indirect(entries(offs_sb, halves[0])))
+        w1s = deal(nc.vector.tensor_copy, "w1s", w1s_raw, U8)
+        nc.vector.tensor_copy(xq_w[:, halves[1]], xw[:].indirect(entries(offs_sb, halves[1])))
         sig_bias = sb("sig_bias", [P, PACK], F32)
-        gain = sb("gain", [P, PACK], F32)
-        neg_tau = sb("neg_tau", [P, PACK], F32)
-        w1s = []
-        for t in tiles:
-            w1s.append(sb(f"w1s_{t}", [P, P], U8))
-            nc.gpsimd.tensor_copy(w1s[t][:], w1s_raw[:, t : S : PACK])
-            if t == 0:
-                nc.gpsimd.tensor_scalar(neg_th[:], th_sb[:], -1.0, 0.0, ALU.mult, ALU.add)
-                nc.gpsimd.tensor_tensor(sig_bias[:], neg_th[:], sl_sb[:], ALU.mult)
-        w3 = deal(nc.gpsimd.tensor_copy, "w3", w3_raw, U32)
-        nc.gpsimd.tensor_scalar(gain[:], gn_sb[:], -1.5, 0.0, ALU.mult, ALU.add)
-        nc.gpsimd.tensor_scalar(neg_tau[:], tau_sb[:], -1.0, 0.0, ALU.mult, ALU.add)
-
-        def rows_of(t):
-            return slice(t * P, (t + 1) * P)
-
-        def product(out, w, ws, x, xsc):
-            nc.tensor.matmul_mx(
-                out=out, lhsT=w.bitcast(FP8X4), lhsT_scale=ws,
-                rhs=x.bitcast(FP8X4), rhs_scale=xsc, start=True, stop=True,
-            )
+        nc.vector.scalar_tensor_tensor(sig_bias[:], sl_sb[:], -1.0, th_sb[:], ALU.mult, ALU.mult)
+        nc.vector.tensor_copy(x2_w[:], xw[:].indirect(two_sb[:]))
+        w3 = deal(nc.scalar.copy, "w3", w3_raw, U32)
 
         z = sb("z", [P, PACK, S], BF16)
-        d = [window(f"d{t}") for t in tiles]
-        hh = {t: window(f"h{t}") for t in (0, 1, last)}
+        d = [window(f"d{t}") for t in row_tiles]
+        h2 = {t: window(f"h2_{t}") for t in (0, 1, LAST)}
 
-        y_ps = [psum.tile([P, S], F32, name="y_ps", tag=f"yh{t}") for t in range(2)]
-        for h in halves:
-            product(y_ps[0][:, cols(h)], w1[:, rows_of(0)], w1s[0][:], xq_w[:, cols(h)], xq_s[:, cols(h)])
-        product(y_ps[1][:], w1[:, rows_of(1)], w1s[1][:], xq_w[:], xq_s[:])
-        nc.scalar.copy(y[0][:, whole], y_ps[0][:])
-        nc.vector.tensor_copy(y[1][:, whole], y_ps[1][:])
-        for t in tiles:
+        def fetch_sg(t, c):
+            nc.scalar.activation(h2[t][:, spare(c)], sg[t][:].indirect(entries(n2_sb, c)), ACT.Copy)
+
+        y_ps = [bank(f"yh{t}") for t in range(LAST)]
+        for c, out in zip(halves, (bank("yh3", HALF)[:], y_ps[0][:, halves[1]])):
+            product(out, w1[:, rows_of(0)], w1s[:, rows_of(0)], xq_w[:, c], xq_s[:, c])
+            nc.scalar.copy(y[0][:, c], out)
+        y_ps.append(bank("yh0"))
+        for t in range(1, PACK):
+            product(y_ps[t][:], w1[:, rows_of(t)], w1s[:, rows_of(t)], xq_w[:], xq_s[:])
+        for t in (1, 2):
+            nc.vector.tensor_copy(y[t][:, whole], y_ps[t][:])
+        for t in row_tiles:
             nc.scalar.activation(
                 sg[t][:, whole], y[t][:].indirect(n1_sb[:]), ACT.Sigmoid,
                 bias=sig_bias[:, t : t + 1], scale=sl_sb[:, t : t + 1],
             )
-            if t < 2:
-                bank = psum.tile([P, S], F32, name="y_ps", tag=f"yh{t}")
-                product(bank[:], w1[:, rows_of(t + 2)], w1s[t + 2][:], xq_w[:], xq_s[:])
-                nc.scalar.copy(y[t + 2][:, whole], bank[:])
-        hh[2] = window("sig_bias")
-        for t, c in ((2, whole), (last, cols(0)), (last, cols(1))):
-            nc.scalar.activation(hh[t][:, spare(c)], sg[t][:].indirect(entries(n2_sb, c)), ACT.Copy)
+            if t == 1:
+                nc.scalar.copy(y[LAST][:, whole], y_ps[LAST][:])
+            if t == 2:
+                fetch_sg(1, whole)
+        h2[2] = window("sig_bias")
+        fetch_sg(2, whole)
+        for c in halves:
+            fetch_sg(LAST, c)
 
-        w3s = deal(nc.gpsimd.tensor_copy, "w1", w3s_raw, U8)
-        w2 = deal(nc.gpsimd.tensor_copy, "w3s_raw", w2_raw, U32)
-        w2s = deal(nc.gpsimd.tensor_copy, "w2_raw", w2s_raw, U8)
-        d_ps = [psum.tile([P, S], F32, name="d_ps", tag=f"d{t}") for t in tiles]
-        for t in tiles:
+        w3s = deal(nc.vector.tensor_copy, "w1", w3s_raw, U8)
+        gain = sb("w3s_raw", [P, PACK], F32)
+        nc.vector.tensor_scalar(gain[:], gn_sb[:], -1.5, None, ALU.mult)
+        d_ps = [bank(f"d_ps{t}") for t in row_tiles]
+        for t in row_tiles:
             product(d_ps[t][:], w3[:, rows_of(t)], w3s[:, rows_of(t)], x2_w[:], x2_s[:])
 
-        z4 = sb("z4", [P, S * PACK], BF16)
-        zw = sb("zw", [P, S], U32)
-        zs = sb("zs", [P, S], U8)
+        exp_bias = sb("exp_bias", [P, PACK], F32)
 
-        def weave(copy, dst, c, src):
-            copy(
-                dst[:, PACK * c.start : PACK * c.stop].rearrange("p (c i t) -> p c t i", i=4, t=PACK),
-                src[:, :, c].rearrange("p t (c i) -> p c t i", i=4),
-            )
+        def d_out(t, top_name):
+            top = sb(top_name, [P, 1], F32)
+            nc.vector.tensor_scalar(d[t][:, whole], d_ps[t][:], 1.0, None, ALU.mult, ALU.max, accum_out=top[:])
+            nc.vector.scalar_tensor_tensor(exp_bias[:, t : t + 1], top[:], -1.0, tau_sb[:, t : t + 1], ALU.mult, ALU.mult)
 
-        def quantise(words, plane, src, c):
-            nc.vector.quantize_mx(
-                out=words[:, c].bitcast(FP8X4), scales=plane[:, c], in_=src[:, PACK * c.start : PACK * c.stop]
-            )
-
-        def gate_difference(t, c):
-            nc.vector.tensor_tensor(d[t][:, spare(c)], hh[t][:, spare(c)], sg[t][:, c], ALU.subtract)
+        def sg_difference(t, c):
+            nc.vector.tensor_tensor(d[t][:, spare(c)], h2[t][:, spare(c)], sg[t][:, c], ALU.subtract)
 
         def z_of(t, c):
             nc.vector.scalar_tensor_tensor(
                 z[:, t, c], d[t][:, spare(c)], gain[:, t : t + 1], y[t][:, c], ALU.mult, ALU.mult
             )
 
-        for t in range(2):
-            nc.vector.tensor_copy(hh[t][:, S:], sg[t][:, whole])
-            nc.vector.tensor_tensor(d[t][:, S:], sg[t][:].indirect(n2_sb[:]), hh[t][:, S:], ALU.subtract)
-            z_of(t, whole)
-        gate_difference(2, whole)
-        gate_difference(last, cols(0))
+        z4 = sb("z4", [P, S * PACK], BF16)
+        zw = sb("zw", [P, S], U32)
+        zs = sb("zs", [P, S], U8)
+        nc.vector.tensor_copy(h2[0][:, S:], sg[0][:, whole])
+        nc.vector.tensor_tensor(d[0][:, S:], sg[0][:].indirect(n2_sb[:]), h2[0][:, S:], ALU.subtract)
+        d_out(0, "top0")
+        z_of(0, whole)
+        d_out(1, "top1")
+        sg_difference(1, whole)
+        z_of(1, whole)
+        d_out(2, "top2")
+        w2 = deal(nc.vector.tensor_copy, "x2_w", w2_raw, U32)
+        w2s = deal(nc.vector.tensor_copy, "x2_s", w2s_raw, U8)
+        sg_difference(2, whole)
+        sg_difference(LAST, halves[0])
         z_of(2, whole)
-        z_of(last, cols(0))
-        gate_difference(last, cols(1))
-        weave(nc.vector.tensor_copy, z4, cols(0), z)
-        z_of(last, cols(1))
-        quantise(zw, zs, z4, cols(0))
-        weave(nc.vector.tensor_copy, z4, cols(1), z)
-        quantise(zw, zs, z4, cols(1))
+        z_of(LAST, halves[0])
+        sg_difference(LAST, halves[1])
+        weave(nc.vector.tensor_copy, z4, z, halves[0])
+        z_of(LAST, halves[1])
+        quantise(zw, zs, z4, halves[0])
+        weave(nc.vector.tensor_copy, z4, z, halves[1])
+        quantise(zw, zs, z4, halves[1])
+        d_out(LAST, "z")
 
-        top = sb("top", [P, last], F32)
-        last_top = sb("z", [P, 1], F32)
-        exp_bias = sb("exp_bias", [P, PACK], F32)
-        for t in tiles:
-            largest = top[:, t : t + 1] if t < last else last_top[:]
-            nc.vector.tensor_scalar(d[t][:, whole], d_ps[t][:], 1.0, None, ALU.mult, ALU.max, accum_out=largest)
-            if t == last - 1:
-                nc.vector.tensor_tensor(exp_bias[:, :last], top[:], neg_tau[:, :last], ALU.mult)
-        nc.vector.tensor_tensor(exp_bias[:, last:], last_top[:], neg_tau[:, last:], ALU.mult)
+        h_ps = [bank(f"yh{t}") for t in row_tiles]
+        for t in row_tiles:
+            for c in halves:
+                product(h_ps[t][:, c], w2[:, rows_of(t)], w2s[:, rows_of(t)], zw[:, c], zs[:, c])
 
-        h_ps = [psum.tile([P, S], F32, name="h_ps", tag=f"yh{t}") for t in tiles]
-        for t in tiles:
-            for h in halves:
-                product(h_ps[t][:, cols(h)], w2[:, rows_of(t)], w2s[:, rows_of(t)], zw[:, cols(h)], zs[:, cols(h)])
-
-        ea = [sb(tag, [P, S], F32) for tag in ("sl_sb", "sg2", "ea2", "ea3")]
-        hg = [sb(f"hg{t}", [P, S], F32) for t in tiles]
-        v = [sb(f"v{t}", [P, S], F32) for t in tiles]
-        m = [sb(f"m{t}", [P, S], F32) for t in tiles]
+        ea = [sb(name, [P, S], F32) for name in ("sl_sb", "sg2", "ea2", "ea3")]
+        h2_at = [sb(f"h2_at{t}", [P, S], F32) for t in row_tiles]
+        step = [sb(f"step{t}", [P, S], F32) for t in row_tiles]
+        weighed = [sb(f"weighed{t}", [P, S], F32) for t in row_tiles]
         res = sb("res", [P, PACK, S], F32)
         res4 = sb("res4", [P, S * PACK], BF16)
-        ow = sb("ow", [P, S], U32)
-        osc = sb("osc", [P, S], U8)
+        out_words = sb("out_words", [P, S], U32)
+        out_plane = sb("out_plane", [P, S], U8)
         out_rows = out_0.rearrange("(p t) j -> p t j", t=PACK)
 
         def exp_of(t, c):
@@ -239,51 +240,58 @@ def tile_picked_latepxbedb_none_po_kernel(
                 bias=exp_bias[:, t : t + 1], scale=tau_sb[:, t : t + 1],
             )
 
-        def fetch(t, c):
-            nc.scalar.activation(hg[t][:, c], hh[t][:].indirect(entries(n4_sb, c)), ACT.Copy)
+        def h_out(t):
+            nc.scalar.activation(h2[t][:, whole], h_ps[t][:], ACT.Copy, scale=-2.0)
 
-        def difference(t, c):
-            nc.vector.scalar_tensor_tensor(v[t][:, c], h_ps[t][:, c], 2.0, hg[t][:, c], ALU.mult, ALU.add)
+        def fetch_h(t, c):
+            nc.scalar.activation(h2_at[t][:, c], h2[t][:].indirect(entries(n4_sb, c)), ACT.Copy)
+
+        def h_difference(t, c):
+            nc.vector.scalar_tensor_tensor(step[t][:, c], h_ps[t][:, c], 2.0, h2_at[t][:, c], ALU.mult, ALU.add)
 
         def weigh(t, c):
-            nc.gpsimd.tensor_tensor(m[t][:, c], v[t][:, c], ea[t][:, c], ALU.mult)
+            nc.vector.tensor_tensor(weighed[t][:, c], step[t][:, c], ea[t][:, c], ALU.mult)
 
         def finish(t, c):
-            nc.vector.scalar_tensor_tensor(res[:, t, c], d_ps[t][:, c], -0.5, m[t][:, c], ALU.mult, ALU.add)
+            nc.vector.scalar_tensor_tensor(res[:, t, c], d_ps[t][:, c], -0.5, weighed[t][:, c], ALU.mult, ALU.add)
 
         def hand_on(c):
-            quantise(ow, osc, res4, c)
-            nc.sync.dma_start(out_1[0].rearrange("p n t -> p (n t)").bitcast(I32)[:, c], ow[:, c].bitcast(I32))
+            quantise(out_words, out_plane, res4, c)
+            nc.sync.dma_start(out_1[0].rearrange("p n t -> p (n t)").bitcast(I32)[:, c], out_words[:, c].bitcast(I32))
 
-        for t in range(2):
+        for t in (0, 1):
             exp_of(t, whole)
-        nc.vector.tensor_scalar(hh[0][:, whole], h_ps[0][:], -2.0, None, ALU.mult)
-        nc.scalar.activation(hh[1][:, whole], h_ps[1][:], ACT.Copy, scale=-2.0)
-        fetch(1, whole)
-        nc.vector.tensor_scalar(hh[2][:, whole], h_ps[2][:], -2.0, None, ALU.mult)
-        nc.vector.tensor_copy(hg[0][:], hh[0][:, whole])
-        nc.vector.tensor_scalar(hh[3][:, whole], h_ps[3][:], -2.0, None, ALU.mult)
-        nc.vector.tensor_tensor(v[0][:], hh[0][:].indirect(n4_sb[:]), hg[0][:], ALU.subtract)
-        for h in halves:
-            for step in (fetch, exp_of):
+        nc.vector.tensor_scalar(h2[0][:, whole], h_ps[0][:], -2.0, None, ALU.mult)
+        h_out(1)
+        fetch_h(1, whole)
+        h_out(2)
+        nc.vector.tensor_copy(h2_at[0][:], h2[0][:, whole])
+        nc.vector.tensor_tensor(step[0][:], h2[0][:].indirect(n4_sb[:]), h2_at[0][:], ALU.subtract)
+        h_out(3)
+        for c in halves:
+            for on_scalar in (fetch_h, exp_of):
                 for t in (2, 3):
-                    step(t, cols(h))
+                    on_scalar(t, c)
         weigh(0, whole)
-        difference(1, whole)
+        h_difference(1, whole)
         weigh(1, whole)
-        for t in range(2):
+        for t in (0, 1):
             finish(t, whole)
         nc.sync.dma_start(out_rows[:, 0:2, :], res[:, 0:2, :])
-        for h in halves:
-            for step in (difference, weigh, finish):
+        for c in halves:
+            for on_vector in (h_difference, weigh, finish):
                 for t in (2, 3):
-                    step(t, cols(h))
-            nc.sync.dma_start(out_rows[:, 2:4, cols(h)], res[:, 2:4, cols(h)])
-        weave(nc.scalar.copy, res4, cols(0), res)
-        hand_on(cols(0))
-        weave(nc.vector.tensor_copy, res4, slice(HALF, SPLIT), res)
-        weave(nc.scalar.copy, res4, slice(SPLIT, S), res)
-        hand_on(cols(1))
-        for q in range(4):
+                    on_vector(t, c)
+            nc.sync.dma_start(out_rows[:, 2:4, c], res[:, 2:4, c])
+
+        weave(nc.scalar.copy, res4, res, halves[0])
+        hand_on(halves[0])
+        weave(nc.vector.tensor_copy, res4, res, slice(HALF, SPLIT))
+        weave(nc.scalar.copy, res4, res, slice(SPLIT, S))
+        hand_on(halves[1])
+        for q in range(P // QUADRANT):
             queue = nc.sync if q % 2 else nc.scalar
-            queue.dma_start(out_2[0, 4 * q : 4 * q + 4, :].bitcast(I32), osc[32 * q : 32 * q + 4, :].bitcast(I32))
+            queue.dma_start(
+                out_2[0, 4 * q : 4 * q + 4, :].bitcast(I32),
+                out_plane[QUADRANT * q : QUADRANT * q + 4, :].bitcast(I32),
+            )

@@ -105,8 +105,13 @@ def tile_picked_latepxbedb_none_po_kernel(
 
         y = [window(f"y{t}") for t in row_tiles]
         sg = [window(f"sg{t}") for t in range(LAST)] + [sb("sg3", [P, S], F32)]
-        for tile in y + sg[:LAST]:
+        for tile in y:
             nc.vector.memset(tile[:, S:], 0.0)
+        for tile in sg[:LAST]:
+            nc.gpsimd.memset(tile[:, S:], 0.0)
+
+        warm = sb("warm", [P, 1], F32)
+        nc.scalar.activation(warm[:], y[0][:, S : S + 1], ACT.Sigmoid)
 
         xs = load_scales("xs", x_scales, T)
         offs_sb = load_list("offs_sb", offs)
@@ -130,15 +135,17 @@ def tile_picked_latepxbedb_none_po_kernel(
         xq_s = sb("xq_s", [P, S], U8)
         xq_w = sb("xq_w", [P, S], U32)
         x2_s = sb("x2_s", [P, S], U8)
-        x2_w = sb("x2_w", [P, S], U32)
         w1 = deal(nc.scalar.copy, "w1", w1_raw, U32)
         nc.vector.tensor_copy(xq_s[:], xs[:].indirect(offs_sb[:]))
         nc.vector.tensor_copy(x2_s[:], xs[:].indirect(two_sb[:]))
         nc.vector.tensor_copy(xq_w[:, halves[0]], xw[:].indirect(entries(offs_sb, halves[0])))
         w1s = deal(nc.vector.tensor_copy, "w1s", w1s_raw, U8)
         nc.vector.tensor_copy(xq_w[:, halves[1]], xw[:].indirect(entries(offs_sb, halves[1])))
+        neg_th = sb("neg_th", [P, PACK], F32)
         sig_bias = sb("sig_bias", [P, PACK], F32)
-        nc.vector.scalar_tensor_tensor(sig_bias[:], sl_sb[:], -1.0, th_sb[:], ALU.mult, ALU.mult)
+        nc.gpsimd.tensor_scalar(neg_th[:], th_sb[:], -1.0, 0.0, ALU.mult, ALU.add)
+        nc.gpsimd.tensor_tensor(sig_bias[:], neg_th[:], sl_sb[:], ALU.mult)
+        x2_w = sb("w1s_raw", [P, S], U32)
         nc.vector.tensor_copy(x2_w[:], xw[:].indirect(two_sb[:]))
         w3 = deal(nc.scalar.copy, "w3", w3_raw, U32)
 
@@ -205,7 +212,7 @@ def tile_picked_latepxbedb_none_po_kernel(
         sg_difference(1, whole)
         z_of(1, whole)
         d_out(2, "top2")
-        w2 = deal(nc.vector.tensor_copy, "x2_w", w2_raw, U32)
+        w2 = deal(nc.vector.tensor_copy, "w1s_raw", w2_raw, U32)
         w2s = deal(nc.vector.tensor_copy, "x2_s", w2s_raw, U8)
         sg_difference(2, whole)
         sg_difference(LAST, halves[0])

from contextlib import ExitStack

import concourse.mybir as mybir

F32 = mybir.dt.float32
BF16 = mybir.dt.bfloat16
U32 = mybir.dt.uint32
I32 = mybir.dt.int32
U16 = mybir.dt.uint16
U8 = mybir.dt.uint8
FP8X4 = mybir.dt.float8_e4m3fn_x4
ALU = mybir.AluOpType
ACT = mybir.ActivationFunctionType

P = 128
PACK = 4
LAST = PACK - 1
T = 2048
S = 512
HALF = S // 2
QUADRANT = 32
PER_COLUMN = 16
SPLIT = 416
FLOPS = 3 * 2 * 512 * 512 * 512


def tile_picked_latepxbedb_none_po_kernel(
    tc, x_words, x_scales, w1_words, w1_scales, sl, th, gn, w2_words, w2_scales, w3_words, w3_scales, tau,
    offs, n1, n2, two, n3, n4, out_0, out_1, out_2,
):
    nc = tc.nc
    row_tiles = range(PACK)
    whole = slice(0, S)
    halves = (slice(0, HALF), slice(HALF, S))

    def entries(lst, c):
        return lst[:, c.start // PER_COLUMN : c.stop // PER_COLUMN]

    def spare(c):
        return slice(S + c.start, S + c.stop)

    def rows_of(t):
        return slice(t * P, (t + 1) * P)

    with ExitStack() as ctx:
        keep = ctx.enter_context(tc.tile_pool(name="keep", bufs=1))
        psum = ctx.enter_context(tc.psum_pool(name="psum", bufs=1))

        def sb(name, shape, dtype):
            return keep.tile(shape, dtype, name=name, align_bytes=64)

        def bank(name, width=S):
            return psum.tile([P, width], F32, name=name)

        def window(name):
            return sb(name, [P, 2 * S], F32)

        def load_list(name, src):
            lst = sb(name, [P, S // PER_COLUMN], U16)
            nc.sync.dma_start(lst[:], src)
            return lst

        def load_words(name, src, width):
            words = sb(name, [P, width], U32)
            nc.sync.dma_start(words[:].bitcast(I32), src[0].rearrange("p n t -> p (n t)").bitcast(I32))
            return words

        def load_scales(name, src, width):
            plane = sb(name, [P, width], U8)
            for q in range(P // QUADRANT):
                rows = src[0, 4 * q : 4 * q + 4, :].bitcast(I32)
                nc.sync.dma_start(
                    plane[QUADRANT * q : QUADRANT * (q + 1), :].bitcast(I32),
                    rows.unsqueeze(0).to_broadcast([QUADRANT // 4, 4, width // 4]),
                )
            return plane

        def load_rows(name, src):
            vec = sb(name, [P, PACK], F32)
            nc.sync.dma_start(vec[:], src.rearrange("(p t) o -> p (t o)", t=PACK))
            return vec

        def deal(copy, name, src, dtype):
            dst = sb(name, [P, S], dtype)
            walk = "p m t" if dtype == U32 else "p t m"
            copy(dst[:].rearrange(f"p (t m) -> {walk}", t=PACK), src[:].rearrange(f"p (m t) -> {walk}", t=PACK))
            return dst

        def product(out, w, w_scale, x, x_scale):
            nc.tensor.matmul_mx(
                out=out, lhsT=w.bitcast(FP8X4), lhsT_scale=w_scale,
                rhs=x.bitcast(FP8X4), rhs_scale=x_scale, start=True, stop=True,
            )

        def weave(copy, dst, src, c):
            copy(
                dst[:, PACK * c.start : PACK * c.stop].rearrange("p (c i t) -> p c t i", i=4, t=PACK),
                src[:, :, c].rearrange("p t (c i) -> p c t i", i=4),
            )

        def quantise(words, plane, woven, c):
            nc.vector.quantize_mx(
                out=words[:, c].bitcast(FP8X4), scales=plane[:, c], in_=woven[:, PACK * c.start : PACK * c.stop]
            )

        y = [window(f"y{t}") for t in row_tiles]
        sg = [window(f"sg{t}") for t in range(LAST)] + [sb("sg3", [P, S], F32)]
        for tile in y:
            nc.vector.memset(tile[:, S:], 0.0)
        for tile in sg[:LAST]:
            nc.gpsimd.memset(tile[:, S:], 0.0)

        warm = sb("warm", [P, 1], F32)
        nc.scalar.activation(warm[:], y[0][:, S : S + 1], ACT.Sigmoid)

        xs = load_scales("xs", x_scales, T)
        offs_sb = load_list("offs_sb", offs)
        two_sb = load_list("two_sb", two)
        w1_raw = load_words("w1_raw", w1_words, S)
        xw = load_words("xw", x_words, T)
        w1s_raw = load_scales("w1s_raw", w1_scales, S)
        sl_sb = load_rows("sl_sb", sl)
        th_sb = load_rows("th_sb", th)
        w3_raw = load_words("w3_raw", w3_words, S)
        n1_sb = load_list("n1_sb", n1)
        w3s_raw = load_scales("w3s_raw", w3_scales, S)
        gn_sb = load_rows("gn_sb", gn)
        n2_sb = load_list("n2_sb", n2)
        tau_sb = load_rows("tau_sb", tau)
        w2_raw = load_words("w2_raw", w2_words, S)
        w2s_raw = load_scales("w2s_raw", w2_scales, S)
        n3_sb = load_list("n3_sb", n3)
        n4_sb = load_list("n4_sb", n4)

        xq_s = sb("xq_s", [P, S], U8)
        xq_w = sb("xq_w", [P, S], U32)
        x2_s = sb("x2_s", [P, S], U8)
        w1 = deal(nc.scalar.copy, "w1", w1_raw, U32)
        nc.vector.tensor_copy(xq_s[:], xs[:].indirect(offs_sb[:]))
        nc.vector.tensor_copy(x2_s[:], xs[:].indirect(two_sb[:]))
        nc.vector.tensor_copy(xq_w[:, halves[0]], xw[:].indirect(entries(offs_sb, halves[0])))
        w1s = deal(nc.vector.tensor_copy, "w1s", w1s_raw, U8)
        nc.vector.tensor_copy(xq_w[:, halves[1]], xw[:].indirect(entries(offs_sb, halves[1])))
        neg_th = sb("neg_th", [P, PACK], F32)
        sig_bias = sb("sig_bias", [P, PACK], F32)
        nc.gpsimd.tensor_scalar(neg_th[:], th_sb[:], -1.0, 0.0, ALU.mult, ALU.add)
        nc.gpsimd.tensor_tensor(sig_bias[:], neg_th[:], sl_sb[:], ALU.mult)
        x2_w = sb("w1s_raw", [P, S], U32)
        nc.vector.tensor_copy(x2_w[:], xw[:].indirect(two_sb[:]))
        w3 = deal(nc.scalar.copy, "w3", w3_raw, U32)

        z = sb("z", [P, PACK, S], BF16)
        d = [window(f"d{t}") for t in row_tiles]
        h2 = {t: window(f"h2_{t}") for t in (0, 1, LAST)}

        def fetch_sg(t, c):
            nc.scalar.activation(h2[t][:, spare(c)], sg[t][:].indirect(entries(n2_sb, c)), ACT.Copy)

        y_ps = [bank(f"yh{t}") for t in range(LAST)]
        for c, out in zip(halves, (bank("yh3", HALF)[:], y_ps[0][:, halves[1]])):
            product(out, w1[:, rows_of(0)], w1s[:, rows_of(0)], xq_w[:, c], xq_s[:, c])
            nc.scalar.copy(y[0][:, c], out)
        y_ps.append(bank("yh0"))
        for t in range(1, PACK):
            product(y_ps[t][:], w1[:, rows_of(t)], w1s[:, rows_of(t)], xq_w[:], xq_s[:])
        for t in (1, 2):
            nc.vector.tensor_copy(y[t][:, whole], y_ps[t][:])
        for t in row_tiles:
            nc.scalar.activation(
                sg[t][:, whole], y[t][:].indirect(n1_sb[:]), ACT.Sigmoid,
                bias=sig_bias[:, t : t + 1], scale=sl_sb[:, t : t + 1],
            )
            if t == 1:
                nc.scalar.copy(y[LAST][:, whole], y_ps[LAST][:])
            if t == 2:
                fetch_sg(1, whole)
        h2[2] = window("sig_bias")
        fetch_sg(2, whole)
        for c in halves:
            fetch_sg(LAST, c)

        w3s = deal(nc.vector.tensor_copy, "w1", w3s_raw, U8)
        gain = sb("w3s_raw", [P, PACK], F32)
        nc.vector.tensor_scalar(gain[:], gn_sb[:], -1.5, None, ALU.mult)
        d_ps = [bank(f"d_ps{t}") for t in row_tiles]
        for t in row_tiles:
            product(d_ps[t][:], w3[:, rows_of(t)], w3s[:, rows_of(t)], x2_w[:], x2_s[:])

        exp_bias = sb("exp_bias", [P, PACK], F32)

        def d_out(t, top_name):
            top = sb(top_name, [P, 1], F32)
            nc.vector.tensor_scalar(d[t][:, whole], d_ps[t][:], 1.0, None, ALU.mult, ALU.max, accum_out=top[:])
            nc.vector.scalar_tensor_tensor(exp_bias[:, t : t + 1], top[:], -1.0, tau_sb[:, t : t + 1], ALU.mult, ALU.mult)

        def sg_difference(t, c):
            nc.vector.tensor_tensor(d[t][:, spare(c)], h2[t][:, spare(c)], sg[t][:, c], ALU.subtract)

        def z_of(t, c):
            nc.vector.scalar_tensor_tensor(
                z[:, t, c], d[t][:, spare(c)], gain[:, t : t + 1], y[t][:, c], ALU.mult, ALU.mult
            )

        z4 = sb("z4", [P, S * PACK], BF16)
        zw = sb("zw", [P, S], U32)
        zs = sb("zs", [P, S], U8)
        nc.vector.tensor_copy(h2[0][:, S:], sg[0][:, whole])
        nc.vector.tensor_tensor(d[0][:, S:], sg[0][:].indirect(n2_sb[:]), h2[0][:, S:], ALU.subtract)
        d_out(0, "top0")
        z_of(0, whole)
        d_out(1, "top1")
        sg_difference(1, whole)
        z_of(1, whole)
        d_out(2, "top2")
        w2 = deal(nc.vector.tensor_copy, "w1s_raw", w2_raw, U32)
        w2s = deal(nc.vector.tensor_copy, "x2_s", w2s_raw, U8)
        sg_difference(2, whole)
        sg_difference(LAST, halves[0])
        z_of(2, whole)
        z_of(LAST, halves[0])
        sg_difference(LAST, halves[1])
        weave(nc.vector.tensor_copy, z4, z, halves[0])
        z_of(LAST, halves[1])
        quantise(zw, zs, z4, halves[0])
        weave(nc.vector.tensor_copy, z4, z, halves[1])
        quantise(zw, zs, z4, halves[1])
        d_out(LAST, "z")

        h_ps = [bank(f"yh{t}") for t in row_tiles]
        for t in row_tiles:
            for c in halves:
                product(h_ps[t][:, c], w2[:, rows_of(t)], w2s[:, rows_of(t)], zw[:, c], zs[:, c])

        ea = [sb(name, [P, S], F32) for name in ("sl_sb", "sg2", "ea2", "ea3")]
        h2_at = [sb(f"h2_at{t}", [P, S], F32) for t in row_tiles]
        step = [sb(f"step{t}", [P, S], F32) for t in row_tiles]
        weighed = [sb(f"weighed{t}", [P, S], F32) for t in row_tiles]
        res = sb("res", [P, PACK, S], F32)
        res4 = sb("res4", [P, S * PACK], BF16)
        out_words = sb("out_words", [P, S], U32)
        out_plane = sb("out_plane", [P, S], U8)
        out_rows = out_0.rearrange("(p t) j -> p t j", t=PACK)

        def exp_of(t, c):
            nc.scalar.activation(
                ea[t][:, c], d[t][:].indirect(entries(n3_sb, c)), ACT.Exp,
                bias=exp_bias[:, t : t + 1], scale=tau_sb[:, t : t + 1],
            )

        def h_out(t):
            nc.scalar.activation(h2[t][:, whole], h_ps[t][:], ACT.Copy, scale=-2.0)

        def fetch_h(t, c):
            nc.scalar.activation(h2_at[t][:, c], h2[t][:].indirect(entries(n4_sb, c)), ACT.Copy)

        def h_difference(t, c):
            nc.vector.scalar_tensor_tensor(step[t][:, c], h_ps[t][:, c], 2.0, h2_at[t][:, c], ALU.mult, ALU.add)

        def weigh(t, c):
            nc.vector.tensor_tensor(weighed[t][:, c], step[t][:, c], ea[t][:, c], ALU.mult)

        def finish(t, c):
            nc.vector.scalar_tensor_tensor(res[:, t, c], d_ps[t][:, c], -0.5, weighed[t][:, c], ALU.mult, ALU.add)

        def hand_on(c):
            quantise(out_words, out_plane, res4, c)
            nc.sync.dma_start(out_1[0].rearrange("p n t -> p (n t)").bitcast(I32)[:, c], out_words[:, c].bitcast(I32))

        for t in (0, 1):
            exp_of(t, whole)
        nc.vector.tensor_scalar(h2[0][:, whole], h_ps[0][:], -2.0, None, ALU.mult)
        h_out(1)
        fetch_h(1, whole)
        h_out(2)
        nc.vector.tensor_copy(h2_at[0][:], h2[0][:, whole])
        nc.vector.tensor_tensor(step[0][:], h2[0][:].indirect(n4_sb[:]), h2_at[0][:], ALU.subtract)
        h_out(3)
        for c in halves:
            for on_scalar in (fetch_h, exp_of):
                for t in (2, 3):
                    on_scalar(t, c)
        weigh(0, whole)
        h_difference(1, whole)
        weigh(1, whole)
        for t in (0, 1):
            finish(t, whole)
        nc.sync.dma_start(out_rows[:, 0:2, :], res[:, 0:2, :])
        for c in halves:
            for on_vector in (h_difference, weigh, finish):
                for t in (2, 3):
                    on_vector(t, c)
            nc.sync.dma_start(out_rows[:, 2:4, c], res[:, 2:4, c])

        weave(nc.scalar.copy, res4, res, halves[0])
        hand_on(halves[0])
        weave(nc.vector.tensor_copy, res4, res, slice(HALF, SPLIT))
        weave(nc.scalar.copy, res4, res, slice(SPLIT, S))
        hand_on(halves[1])
        for q in range(P // QUADRANT):
            queue = nc.sync if q % 2 else nc.scalar
            queue.dma_start(
                out_2[0, 4 * q : 4 * q + 4, :].bitcast(I32),
                out_plane[QUADRANT * q : QUADRANT * q + 4, :].bitcast(I32),
            )
